import numpy as np
import ml_dtypes


def mxq(x, axis, fmt="e4m3"):
    dtype, down = {"e4m3": (ml_dtypes.float8_e4m3fn, 7), "e5m2": (ml_dtypes.float8_e5m2, 14)}[fmt]
    v = np.moveaxis(np.asarray(x, np.float32).astype(ml_dtypes.bfloat16).astype(np.float64), axis, -1)
    blocks = v.reshape(v.shape[:-1] + (-1, 32))
    amax = np.abs(blocks).max(-1, keepdims=True)
    byte = np.maximum(np.where(amax > 0, np.frexp(amax)[1] - 1 + 127, 0) - down, 1)
    scale = np.exp2(byte - 127.0)
    codes = (blocks / scale).astype(np.float32).astype(dtype).astype(np.float64)
    return np.moveaxis((codes * scale).reshape(v.shape), -1, axis)


WIDE = False


def mx_kscale(k):
    if not WIDE:
        return np.ones(k)
    levels = np.array([10, -10, 5, -5, 0])
    if k % 512:
        return np.exp2(np.random.permutation(np.resize(levels, k // 32))).repeat(32)
    a = np.empty((k // 512, 16))
    for p in range(k // 512):
        a[p, :8] = np.random.permutation(np.resize(levels, 8))
        for g in range(8):
            far = levels[np.abs(levels - a[p, g]) >= 10]
            a[p, g + 8] = far[np.random.randint(len(far))]
    return np.exp2(a.ravel()).repeat(32)


def f64(x):
    return np.asarray(x).astype(np.float64)


def striped(idx):
    return np.tile(idx.reshape(-1, 16).T, (8, 1)).astype(np.uint16)


def unstriped(offs):
    return offs[:16].T.reshape(-1).astype(np.int64)


def striped8(idx):
    return np.concatenate([x.reshape(-1, 16).T for x in idx]).astype(np.uint16)


def runs(offs, k):
    lists = np.stack([offs[16 * r : 16 * r + 16].T.reshape(-1) for r in range(8)]).astype(np.int64)
    return lists[np.arange(k) % 512 // 64]


def pack_weight(w):
    k, n = w.shape
    w = f64(np.asarray(w, np.float32).astype(ml_dtypes.bfloat16)).reshape(k // 32, 32, n)
    amax = np.abs(w).max(1)
    byte = np.clip(np.where(amax > 0, np.frexp(amax)[1] - 1 + 127 - 7, 1), 1, 254)
    scaled = (w * np.exp2(127.0 - byte)[:, None, :]).reshape(k, n).astype(np.float32)
    words = np.ascontiguousarray(scaled.reshape(k // 512, 128, 4, n).transpose(0, 1, 3, 2)).astype(ml_dtypes.float8_e4m3fn).view(np.uint8)
    return words, np.ascontiguousarray(byte.astype(np.uint8).reshape(k // 512, 16, n))


def unpack_weight(words, scales):
    g, p, n, _ = words.shape
    vals = np.ascontiguousarray(words).view(ml_dtypes.float8_e4m3fn).astype(np.float64) * np.repeat(np.exp2(scales.astype(np.float64) - 127.0), 8, axis=1)[..., None]
    return vals.transpose(0, 1, 3, 2).reshape(g * 512, n)


K, T, S, N, H = 512, 2048, 512, 512, 512


def setup_inputs():
    n = np.random.standard_normal
    s = mx_kscale(K)[:, None]
    u = mx_kscale(H)
    packed_xT = pack_weight(n((K, T)) * s)
    return {
        "x_words": packed_xT[0],
        "x_scales": packed_xT[1],
        "w1": (n((K, H)) / np.sqrt(K) / s).astype(np.float32),
        "w2": (n((K, H)) / np.sqrt(K) / s).astype(np.float32),
        "gn": (np.random.uniform(0.5, 1.5, (H, 1)) * u[:, None]).astype(np.float32),
        "gm": (np.random.uniform(0.5, 1.5, (H, 1)) * u[:, None]).astype(np.float32),
        "w3": (n((H, N)) / np.sqrt(2 * H) / u[:, None]).astype(np.float32),
        "w4": (n((H, N)) / np.sqrt(2 * H) / u[:, None]).astype(np.float32),
        "offs": striped(np.random.permutation(T)[:S]),
        "hz": striped8(np.random.randint(0, T, (8, S))),
        "n1": striped(np.random.permutation(S)),
        "n2": striped(np.random.permutation(S)),
        "n3": striped(np.random.permutation(S)),
        "n4": striped(np.random.permutation(S)),
        "n5": striped(np.random.permutation(S)),
    }


def reference(x_words, x_scales, w1, w2, gn, gm, w3, w4, offs, hz, n1, n2, n3, n4, n5):
    xq = unpack_weight(x_words, x_scales)[:, unstriped(offs)]
    y = mxq(f64(w1), 0, "e4m3").T @ xq
    pa = y[:, unstriped(n1)]
    z = f64(gn) * ((2.0 * (y * pa)) / ((y) ** 2 + (pa) ** 2 + 0.5))
    x_hz = unpack_weight(x_words, x_scales)[np.arange(K)[:, None], runs(hz, K)]
    d = mxq(f64(w2), 0, "e4m3").T @ x_hz
    z2 = f64(gm) * (d / (np.abs(d[:, unstriped(n2)]) + 0.5))
    h = mxq(f64(w3), 0, "e4m3").T @ mxq(z, 0, "e4m3") + mxq(f64(w4), 0, "e4m3").T @ mxq(z2, 0, "e4m3")
    return 0.75 * (h * h[:, unstriped(n3)] + h[:, unstriped(n4)] * h[:, unstriped(n5)])

@@ -1,0 +1,194 @@
+from contextlib import ExitStack
+
+import concourse.mybir as mybir
+
+K, T, S, H, N = 512, 2048, 512, 512, 512
+FLOPS = 4 * 2 * 512 * 512 * 512
+
+F32 = mybir.dt.float32
+BF16 = mybir.dt.bfloat16
+I32 = mybir.dt.int32
+U32 = mybir.dt.uint32
+U16 = mybir.dt.uint16
+U8 = mybir.dt.uint8
+FP8X4 = mybir.dt.float8_e4m3fn_x4
+ACT = mybir.ActivationFunctionType
+ALU = mybir.AluOpType
+
+P = 128
+PACK = 4
+WINDOW = 704
+
+
+def tile_picked_hjoinharmnormdot_none_p_kernel(
+    tc, x_words, x_scales, w1, w2, gn, gm, w3, w4, offs, hz, n1, n2, n3, n4, n5, out
+):
+    nc = tc.nc
+    with ExitStack() as ctx:
+        keep = ctx.enter_context(tc.tile_pool(name="keep", bufs=1))
+        psum = ctx.enter_context(tc.psum_pool(name="psum", bufs=1))
+
+        def sb(name, shape, dtype, tag=None):
+            return keep.tile(shape, dtype, name=name, tag=tag or name, align_bytes=64)
+
+        def load_list(name, src):
+            tile = keep.tile([P, S // 16], U16, name=name, tag=name)
+            nc.sync.dma_start(tile[:], src)
+            return tile
+
+        def load_weight(name, src, tag):
+            raw = sb(name, [P, PACK, 512], F32, tag=tag)
+            nc.sync.dma_start(out=raw[:], in_=src.rearrange("(p j) c -> p j c", j=PACK))
+            return raw
+
+        xs = sb("xs", [P, T], U8)
+        scale_rows = x_scales[0].bitcast(I32)
+        for q in range(4):
+            nc.sync.dma_start(
+                out=xs[32 * q : 32 * q + 32, :].bitcast(I32),
+                in_=scale_rows[4 * q : 4 * q + 4, :].unsqueeze(0).to_broadcast([8, 4, T // 4]),
+            )
+        offs_t = load_list("offs_t", offs)
+        hz_t = load_list("hz_t", hz)
+        w1_raw = load_weight("w1_raw", w1, "raw_a")
+        xw = sb("xw", [P, T], I32)
+        nc.sync.dma_start(out=xw[:], in_=x_words[0].rearrange("p n t -> p (n t)").bitcast(I32))
+        w2_raw = load_weight("w2_raw", w2, "raw_b")
+        n1_t = load_list("n1_t", n1)
+        n2_t = load_list("n2_t", n2)
+        n3_t = load_list("n3_t", n3)
+        n4_t = load_list("n4_t", n4)
+        n5_t = load_list("n5_t", n5)
+        gn_t = sb("gn_t", [P, PACK], F32)
+        gm_t = sb("gm_t", [P, PACK], F32)
+        nc.gpsimd.dma_start(out=gn_t[:], in_=gn.rearrange("(p t) o -> p (t o)", t=PACK))
+        nc.gpsimd.dma_start(out=gm_t[:], in_=gm.rearrange("(p t) o -> p (t o)", t=PACK))
+
+        win_a = [sb("win_a%d" % t, [P, WINDOW], F32) for t in range(PACK)]
+        win_b = [sb("win_b%d" % t, [P, WINDOW], F32) for t in range(PACK)]
+        for w in win_a + win_b:
+            nc.gpsimd.memset(w[:, S:], 0.0)
+
+        def cast(raw, name, dealt, cut):
+            grouped = sb(name, [P, 512 * PACK], BF16)
+            if dealt:
+                dst = grouped[:].rearrange("p (t m j) -> p m j t", t=PACK, j=PACK)
+            else:
+                dst = grouped[:].rearrange("p (m t j) -> p m j t", t=PACK, j=PACK)
+            src = raw[:].rearrange("p j (m t) -> p m j t", t=PACK)
+            if cut > 0:
+                nc.vector.tensor_copy(out=dst[:, :cut], in_=src[:, :cut])
+            for a in range(cut, P, 32):
+                b = min(a + 32, P)
+                nc.scalar.copy(out=dst[:, a:b], in_=src[:, a:b])
+            return grouped
+
+        def quantize(grouped, name):
+            codes = sb(name + "_codes", [P, 512], U32)
+            scales = sb(name + "_scales", [P, 512], U8)
+            nc.vector.quantize_mx(out=codes[:].bitcast(FP8X4), scales=scales[:], in_=grouped[:])
+            return codes, scales
+
+        def product(bank, weight, t, moving, start, stop):
+            cols = slice(P * t, P * (t + 1))
+            nc.tensor.matmul_mx(
+                out=bank[:],
+                lhsT=weight[0][:, cols].bitcast(FP8X4),
+                lhsT_scale=weight[1][:, cols],
+                rhs=moving[0][:].bitcast(FP8X4),
+                rhs_scale=moving[1][:],
+                start=start,
+                stop=stop,
+            )
+
+        tok_scales = sb("tok_scales", [P, S], U8)
+        nc.vector.tensor_copy(out=tok_scales[:], in_=xs[:].indirect(offs_t[:]))
+        hz_bytes = sb("hz_bytes", [P, S], U8)
+        nc.vector.tensor_copy(out=hz_bytes[:], in_=xs[:].indirect(hz_t[:]))
+        hz_scales = sb("hz_scales", [P, S], U8)
+        nc.vector.tensor_copy(out=hz_scales[:].bitcast(I32), in_=hz_bytes[:].bitcast(I32))
+        for r in (2, 3):
+            nc.sync.dma_start(out=hz_scales[r:P:32, :].bitcast(I32), in_=hz_bytes[16 + r : P : 32, :].bitcast(I32))
+
+        w1_q = quantize(cast(w1_raw, "w1_bf", True, 96), "w1")
+        w3_raw = load_weight("w3_raw", w3, "raw_a")
+        tok_words = sb("tok_words", [P, S], U32)
+        nc.vector.tensor_copy(out=tok_words[:], in_=xw[:].bitcast(U32).indirect(offs_t[:]))
+        y_ps = [psum.tile([P, S], F32, name="y%d" % t, tag="bank%d" % t) for t in range(PACK)]
+        for t in range(PACK):
+            product(y_ps[t], w1_q, t, (tok_words, tok_scales), True, True)
+
+        hz_words = sb("hz_words", [P, S], U32)
+        nc.vector.tensor_copy(out=hz_words[:], in_=xw[:].bitcast(U32).indirect(hz_t[:]))
+        w2_q = quantize(cast(w2_raw, "w2_bf", True, P), "w2")
+        w4_raw = load_weight("w4_raw", w4, "raw_b")
+        d_ps = [psum.tile([P, S], F32, name="d%d" % t, tag="bank%d" % (PACK + t)) for t in range(PACK)]
+        for t in range(PACK):
+            product(d_ps[t], w2_q, t, (hz_words, hz_scales), True, True)
+
+        def weave(name, left, right):
+            grouped = sb(name, [P, S * PACK], BF16)
+            nc.vector.tensor_tensor(
+                out=grouped[:].rearrange("p (c i t) -> p c t i", i=4, t=PACK),
+                in0=left[:].rearrange("p t (c i) -> p c t i", i=4),
+                in1=right[:].rearrange("p t (c i) -> p c t i", i=4),
+                op=ALU.mult,
+            )
+            return grouped
+
+        pa = sb("pa", [P, PACK, S], F32)
+        y_sq = sb("y_sq", [P, PACK, S], F32)
+        pa_sq = sb("pa_sq", [P, PACK, S], F32)
+        num = sb("num", [P, PACK, S], F32)
+        den = sb("den", [P, PACK, S], F32)
+        root = sb("root", [P, PACK, S], F32)
+        recip = sb("recip", [P, PACK, S], F32)
+        for t in range(PACK):
+            nc.scalar.copy(out=win_a[t][:, :S], in_=y_ps[t][:])
+            nc.scalar.activation(out=pa[:, t, :], in_=win_a[t][:].indirect(n1_t[:]), func=ACT.Copy)
+            nc.scalar.activation(out=y_sq[:, t, :], in_=y_ps[t][:], func=ACT.Square)
+            nc.scalar.activation(out=pa_sq[:, t, :], in_=pa[:, t, :], func=ACT.Square)
+            nc.vector.scalar_tensor_tensor(
+                out=num[:, t, :], in0=y_ps[t][:], scalar=gn_t[:, t : t + 1], in1=pa[:, t, :], op0=ALU.mult, op1=ALU.mult
+            )
+            nc.vector.tensor_tensor(out=den[:, t, :], in0=y_sq[:, t, :], in1=pa_sq[:, t, :], op=ALU.add)
+            nc.scalar.activation(out=root[:, t, :], in_=den[:, t, :], func=ACT.Abs_reciprocal_sqrt, scale=0.5, bias=0.25)
+            nc.scalar.activation(out=recip[:, t, :], in_=root[:, t, :], func=ACT.Square)
+        w3_q = quantize(cast(w3_raw, "w3_bf", False, P), "w3")
+        z_q = quantize(weave("z_bf", num, recip), "z")
+        h_ps = [psum.tile([P, S], F32, name="h%d" % t, tag="bank%d" % t) for t in range(PACK)]
+        for t in range(PACK):
+            product(h_ps[t], w3_q, t, z_q, True, False)
+
+        d_abs = sb("d_abs", [P, PACK, S], F32)
+        s_g = sb("s_g", [P, PACK, S], F32)
+        d_s = sb("d_s", [P, PACK, S], F32)
+        for t in range(PACK):
+            nc.scalar.activation(out=d_abs[:, t, :], in_=d_ps[t][:], func=ACT.Abs)
+            nc.scalar.activation(out=win_b[t][:, :S], in_=d_abs[:, t, :], func=ACT.Abs_reciprocal_sqrt, bias=0.5)
+            nc.vector.tensor_copy(out=s_g[:, t, :], in_=win_b[t][:].indirect(n2_t[:]))
+            nc.vector.scalar_tensor_tensor(
+                out=d_s[:, t, :], in0=d_ps[t][:], scalar=gm_t[:, t : t + 1], in1=s_g[:, t, :], op0=ALU.mult, op1=ALU.mult
+            )
+        z2_bf = weave("z2_bf", d_s, s_g)
+        w4_q = quantize(cast(w4_raw, "w4_bf", False, 0), "w4")
+        z2_q = quantize(z2_bf, "z2")
+        for t in range(PACK):
+            product(h_ps[t], w4_q, t, z2_q, False, True)
+
+        for t in range(PACK):
+            g3 = sb("g3_%d" % t, [P, S], F32)
+            g4 = sb("g4_%d" % t, [P, S], F32)
+            first = sb("first_%d" % t, [P, S], F32)
+            second = sb("second_%d" % t, [P, S], F32)
+            res = sb("res_%d" % t, [P, S], F32)
+            nc.scalar.copy(out=win_a[t][:, :S], in_=h_ps[t][:])
+            if t == 0:
+                nc.vector.tensor_copy(out=g4[:], in_=win_a[t][:].indirect(n4_t[:]))
+            else:
+                nc.scalar.activation(out=g4[:], in_=win_a[t][:].indirect(n4_t[:]), func=ACT.Copy)
+            nc.scalar.activation(out=g3[:], in_=win_a[t][:].indirect(n3_t[:]), func=ACT.Copy)
+            nc.vector.tensor_tensor(out=second[:], in0=win_a[t][:].indirect(n5_t[:]), in1=g4[:], op=ALU.mult)
+            nc.vector.scalar_tensor_tensor(out=first[:], in0=h_ps[t][:], scalar=0.75, in1=g3[:], op0=ALU.mult, op1=ALU.mult)
+            nc.vector.scalar_tensor_tensor(out=res[:], in0=second[:], scalar=0.75, in1=first[:], op0=ALU.mult, op1=ALU.add)
+            nc.sync.dma_start(out=out[P * t : P * (t + 1), :], in_=res[:])

@@ -37,128 +37,136 @@ def tile_picked_hjoinharmnormdot_none_p_kernel(
             return tile
 
         def load_weight(name, src, tag):
-            raw = sb(name, [P, PACK, 512], F32, tag=tag)
+            raw = sb(name, [P, PACK, src.shape[1]], F32, tag=tag)
             nc.sync.dma_start(out=raw[:], in_=src.rearrange("(p j) c -> p j c", j=PACK))
             return raw
 
         xs = sb("xs", [P, T], U8)
-        scale_rows = x_scales[0].bitcast(I32)
-        for q in range(4):
-            nc.sync.dma_start(
-                out=xs[32 * q : 32 * q + 32, :].bitcast(I32),
-                in_=scale_rows[4 * q : 4 * q + 4, :].unsqueeze(0).to_broadcast([8, 4, T // 4]),
-            )
-        offs_t = load_list("offs_t", offs)
+        nc.sync.dma_start(out=xs[:].bitcast(I32), in_=x_scales[0].bitcast(I32).unsqueeze(1).to_broadcast([16, 8, T // 4]))
         hz_t = load_list("hz_t", hz)
-        w1_raw = load_weight("w1_raw", w1, "raw_a")
+        offs_t = load_list("offs_t", offs)
+        n2_t = load_list("n2_t", n2)
+        n1_t = load_list("n1_t", n1)
         xw = sb("xw", [P, T], I32)
         nc.sync.dma_start(out=xw[:], in_=x_words[0].rearrange("p n t -> p (n t)").bitcast(I32))
-        w2_raw = load_weight("w2_raw", w2, "raw_b")
-        n1_t = load_list("n1_t", n1)
-        n2_t = load_list("n2_t", n2)
+        w2_lo = load_weight("w2_lo", w2[:, :256], "raw_c")
+        w2_hi = load_weight("w2_hi", w2[:, 256:], "raw_a")
+        w1_raw = load_weight("w1_raw", w1, "raw_b")
         n3_t = load_list("n3_t", n3)
         n4_t = load_list("n4_t", n4)
         n5_t = load_list("n5_t", n5)
         gn_t = sb("gn_t", [P, PACK], F32)
         gm_t = sb("gm_t", [P, PACK], F32)
-        nc.gpsimd.dma_start(out=gn_t[:], in_=gn.rearrange("(p t) o -> p (t o)", t=PACK))
         nc.gpsimd.dma_start(out=gm_t[:], in_=gm.rearrange("(p t) o -> p (t o)", t=PACK))
+        nc.gpsimd.dma_start(out=gn_t[:], in_=gn.rearrange("(p t) o -> p (t o)", t=PACK))
 
         win_a = [sb("win_a%d" % t, [P, WINDOW], F32) for t in range(PACK)]
         win_b = [sb("win_b%d" % t, [P, WINDOW], F32) for t in range(PACK)]
         for w in win_a + win_b:
-            nc.gpsimd.memset(w[:, S:], 0.0)
+            nc.vector.memset(w[:, S:], 0.0)
 
-        def cast(raw, name, dealt, cut):
-            grouped = sb(name, [P, 512 * PACK], BF16)
+        warm_in = sb("warm_in", [P, 8], F32)
+        warm_out = sb("warm_out", [P, 8], F32)
+        nc.vector.memset(warm_in[:], 1.0)
+        nc.scalar.activation(out=warm_out[:], in_=warm_in[:], func=ACT.Abs_reciprocal_sqrt)
+
+        def cast(grouped, raw, dealt, first, cut):
             if dealt:
                 dst = grouped[:].rearrange("p (t m j) -> p m j t", t=PACK, j=PACK)
             else:
                 dst = grouped[:].rearrange("p (m t j) -> p m j t", t=PACK, j=PACK)
             src = raw[:].rearrange("p j (m t) -> p m j t", t=PACK)
+            groups = src.shape[1]
             if cut > 0:
-                nc.vector.tensor_copy(out=dst[:, :cut], in_=src[:, :cut])
-            for a in range(cut, P, 32):
-                b = min(a + 32, P)
-                nc.scalar.copy(out=dst[:, a:b], in_=src[:, a:b])
-            return grouped
+                nc.vector.tensor_copy(out=dst[:, first : first + cut], in_=src[:, :cut])
+            for a in range(cut, groups, 32):
+                nc.scalar.copy(out=dst[:, first + a : first + a + 32], in_=src[:, a : a + 32])
 
         def quantize(grouped, name):
-            codes = sb(name + "_codes", [P, 512], U32)
-            scales = sb(name + "_scales", [P, 512], U8)
-            nc.vector.quantize_mx(out=codes[:].bitcast(FP8X4), scales=scales[:], in_=grouped[:])
+            width = grouped.shape[1] // PACK
+            codes = sb(name + "_codes", [P, width], U32)
+            scales = sb(name + "_scales", [P, width], U8)
+            nc.vector.quantize_mx(out=codes[:].bitcast(FP8X4), scales=scales[:], in_=grouped)
             return codes, scales
 
-        def product(bank, weight, t, moving, start, stop):
-            cols = slice(P * t, P * (t + 1))
+        def product(acc, weight, wcols, moving, mcols, start, stop):
             nc.tensor.matmul_mx(
-                out=bank[:],
-                lhsT=weight[0][:, cols].bitcast(FP8X4),
-                lhsT_scale=weight[1][:, cols],
-                rhs=moving[0][:].bitcast(FP8X4),
-                rhs_scale=moving[1][:],
+                out=acc,
+                lhsT=weight[0][:, wcols].bitcast(FP8X4),
+                lhsT_scale=weight[1][:, wcols],
+                rhs=moving[0][:, mcols].bitcast(FP8X4),
+                rhs_scale=moving[1][:, mcols],
                 start=start,
                 stop=stop,
             )
 
-        tok_scales = sb("tok_scales", [P, S], U8)
-        nc.vector.tensor_copy(out=tok_scales[:], in_=xs[:].indirect(offs_t[:]))
-        hz_bytes = sb("hz_bytes", [P, S], U8)
-        nc.vector.tensor_copy(out=hz_bytes[:], in_=xs[:].indirect(hz_t[:]))
-        hz_scales = sb("hz_scales", [P, S], U8)
-        nc.vector.tensor_copy(out=hz_scales[:].bitcast(I32), in_=hz_bytes[:].bitcast(I32))
-        for r in (2, 3):
-            nc.sync.dma_start(out=hz_scales[r:P:32, :].bitcast(I32), in_=hz_bytes[16 + r : P : 32, :].bitcast(I32))
+        def block(t):
+            return slice(P * t, P * (t + 1))
 
-        w1_q = quantize(cast(w1_raw, "w1_bf", True, 96), "w1")
-        w3_raw = load_weight("w3_raw", w3, "raw_a")
-        tok_words = sb("tok_words", [P, S], U32)
-        nc.vector.tensor_copy(out=tok_words[:], in_=xw[:].bitcast(U32).indirect(offs_t[:]))
-        y_ps = [psum.tile([P, S], F32, name="y%d" % t, tag="bank%d" % t) for t in range(PACK)]
-        for t in range(PACK):
-            product(y_ps[t], w1_q, t, (tok_words, tok_scales), True, True)
+        every = slice(0, S)
 
-        hz_words = sb("hz_words", [P, S], U32)
-        nc.vector.tensor_copy(out=hz_words[:], in_=xw[:].bitcast(U32).indirect(hz_t[:]))
-        w2_q = quantize(cast(w2_raw, "w2_bf", True, P), "w2")
-        w4_raw = load_weight("w4_raw", w4, "raw_b")
-        d_ps = [psum.tile([P, S], F32, name="d%d" % t, tag="bank%d" % (PACK + t)) for t in range(PACK)]
-        for t in range(PACK):
-            product(d_ps[t], w2_q, t, (hz_words, hz_scales), True, True)
+        def gather(on_vector, dst, window, offsets):
+            if on_vector:
+                nc.vector.tensor_copy(out=dst, in_=window[:].indirect(offsets))
+            else:
+                nc.scalar.activation(out=dst, in_=window[:].indirect(offsets), func=ACT.Copy)
 
-        def weave(name, left, right):
-            grouped = sb(name, [P, S * PACK], BF16)
+        def weave(dst, left, right):
             nc.vector.tensor_tensor(
-                out=grouped[:].rearrange("p (c i t) -> p c t i", i=4, t=PACK),
-                in0=left[:].rearrange("p t (c i) -> p c t i", i=4),
-                in1=right[:].rearrange("p t (c i) -> p c t i", i=4),
+                out=dst.rearrange("p (c i t) -> p c t i", i=4, t=PACK),
+                in0=left.rearrange("p t (c i) -> p c t i", i=4),
+                in1=right.rearrange("p t (c i) -> p c t i", i=4),
                 op=ALU.mult,
             )
-            return grouped
 
-        pa = sb("pa", [P, PACK, S], F32)
-        y_sq = sb("y_sq", [P, PACK, S], F32)
-        pa_sq = sb("pa_sq", [P, PACK, S], F32)
-        num = sb("num", [P, PACK, S], F32)
-        den = sb("den", [P, PACK, S], F32)
-        root = sb("root", [P, PACK, S], F32)
-        recip = sb("recip", [P, PACK, S], F32)
+        def square(on_vector, dst, src, twin):
+            if on_vector:
+                nc.vector.tensor_tensor(out=dst, in0=src, in1=twin, op=ALU.mult)
+            else:
+                nc.scalar.activation(out=dst, in_=src, func=ACT.Square)
+
+        def evacuate(on_vector, dst, src):
+            if on_vector:
+                nc.vector.tensor_copy(out=dst, in_=src)
+            else:
+                nc.scalar.copy(out=dst, in_=src)
+
+        def cast_pool(grouped, raw):
+            dst = grouped[:].rearrange("p (c j) -> p c j", j=PACK)
+            src = raw[:].rearrange("p j c -> p c j")
+            for a in range(0, 512, 128):
+                nc.gpsimd.tensor_scalar(
+                    out=dst[:, a : a + 128], in0=src[:, a : a + 128], scalar1=1.0, scalar2=0.0, op0=ALU.mult, op1=ALU.add
+                )
+
+        picked_bytes = sb("picked_bytes", [P, 2 * S], U8)
+        nc.vector.tensor_copy(out=picked_bytes[:, :S], in_=xs[:].indirect(hz_t[:]))
+        nc.vector.tensor_copy(out=picked_bytes[:, S:], in_=xs[:].indirect(offs_t[:]))
+        x_planes = sb("x_planes", [P, 2 * S], U8)
+        nc.vector.tensor_copy(out=x_planes[:].bitcast(I32), in_=picked_bytes[:].bitcast(I32))
+        for r in (1, 2, 3):
+            nc.scalar.dma_start(out=x_planes[r:P:32, :].bitcast(I32), in_=picked_bytes[8 * r : P : 32, :].bitcast(I32))
+        hz_words = sb("hz_words", [P, S], U32)
+        nc.vector.tensor_copy(out=hz_words[:], in_=xw[:].bitcast(U32).indirect(hz_t[:]))
+        w2_bf = sb("w2_bf", [P, 512 * PACK], BF16)
+        cast(w2_bf, w2_lo, True, 0, 0)
+        cast(w2_bf, w2_hi, True, 64, 0)
+        w3_raw = load_weight("w3_raw", w3, "raw_a")
+        d_ps = [psum.tile([P, S], F32, name="d%d" % t, tag="bank%d" % (PACK + t)) for t in range(PACK)]
         for t in range(PACK):
-            nc.scalar.copy(out=win_a[t][:, :S], in_=y_ps[t][:])
-            nc.scalar.activation(out=pa[:, t, :], in_=win_a[t][:].indirect(n1_t[:]), func=ACT.Copy)
-            nc.scalar.activation(out=y_sq[:, t, :], in_=y_ps[t][:], func=ACT.Square)
-            nc.scalar.activation(out=pa_sq[:, t, :], in_=pa[:, t, :], func=ACT.Square)
-            nc.vector.scalar_tensor_tensor(
-                out=num[:, t, :], in0=y_ps[t][:], scalar=gn_t[:, t : t + 1], in1=pa[:, t, :], op0=ALU.mult, op1=ALU.mult
-            )
-            nc.vector.tensor_tensor(out=den[:, t, :], in0=y_sq[:, t, :], in1=pa_sq[:, t, :], op=ALU.add)
-            nc.scalar.activation(out=root[:, t, :], in_=den[:, t, :], func=ACT.Abs_reciprocal_sqrt, scale=0.5, bias=0.25)
-            nc.scalar.activation(out=recip[:, t, :], in_=root[:, t, :], func=ACT.Square)
-        w3_q = quantize(cast(w3_raw, "w3_bf", False, P), "w3")
-        z_q = quantize(weave("z_bf", num, recip), "z")
-        h_ps = [psum.tile([P, S], F32, name="h%d" % t, tag="bank%d" % t) for t in range(PACK)]
+            w2_q = quantize(w2_bf[:, 512 * t : 512 * (t + 1)], "w2_%d" % t)
+            product(d_ps[t][:], w2_q, block(0), (hz_words, x_planes[:, :S]), every, True, True)
+
+        tok_words = sb("tok_words", [P, S], U32)
+        nc.vector.tensor_copy(out=tok_words[:], in_=xw[:].bitcast(U32).indirect(offs_t[:]))
+        w1_bf = sb("w1_bf", [P, 512 * PACK], BF16)
+        cast(w1_bf, w1_raw, True, 0, P)
+        w1_q = quantize(w1_bf[:], "w1")
+        w4_raw = load_weight("w4_raw", w4, "raw_b")
+
+        y_ps = [psum.tile([P, S], F32, name="y%d" % t, tag="bank%d" % t) for t in range(PACK)]
         for t in range(PACK):
-            product(h_ps[t], w3_q, t, z_q, True, False)
+            product(y_ps[t][:], w1_q, block(t), (tok_words, x_planes[:, S:]), every, True, True)
 
         d_abs = sb("d_abs", [P, PACK, S], F32)
         s_g = sb("s_g", [P, PACK, S], F32)
@@ -166,29 +174,81 @@ def tile_picked_hjoinharmnormdot_none_p_kernel(
         for t in range(PACK):
             nc.scalar.activation(out=d_abs[:, t, :], in_=d_ps[t][:], func=ACT.Abs)
             nc.scalar.activation(out=win_b[t][:, :S], in_=d_abs[:, t, :], func=ACT.Abs_reciprocal_sqrt, bias=0.5)
-            nc.vector.tensor_copy(out=s_g[:, t, :], in_=win_b[t][:].indirect(n2_t[:]))
+            gather("SVVV"[t] == "V", s_g[:, t, :], win_b[t], n2_t[:])
             nc.vector.scalar_tensor_tensor(
                 out=d_s[:, t, :], in0=d_ps[t][:], scalar=gm_t[:, t : t + 1], in1=s_g[:, t, :], op0=ALU.mult, op1=ALU.mult
             )
-        z2_bf = weave("z2_bf", d_s, s_g)
-        w4_q = quantize(cast(w4_raw, "w4_bf", False, 0), "w4")
-        z2_q = quantize(z2_bf, "z2")
+        z2_bf = sb("z2_bf", [P, S * PACK], BF16)
+        for c in range(4):
+            weave(z2_bf[:, 512 * c : 512 * (c + 1)], d_s[:, :, block(c)], s_g[:, :, block(c)])
+        z2_q = quantize(z2_bf[:], "z2")
+
+        pa = sb("pa", [P, PACK, S], F32)
+        y_sq = sb("y_sq", [P, PACK, S], F32)
+        pa_sq = sb("pa_sq", [P, PACK, S], F32)
+        num = sb("num", [P, PACK, S], F32)
+        den = sb("den", [P, PACK, S], F32)
         for t in range(PACK):
-            product(h_ps[t], w4_q, t, z2_q, False, True)
+            evacuate("SSSS"[t] == "V", win_a[t][:, :S], y_ps[t][:])
+            gather("SSSS"[t] == "V", pa[:, t, :], win_a[t], n1_t[:])
+            square("SSSS"[t] == "V", y_sq[:, t, :], y_ps[t][:], win_a[t][:, :S])
+            square("SSSS"[t] == "V", pa_sq[:, t, :], pa[:, t, :], pa[:, t, :])
+            nc.vector.scalar_tensor_tensor(
+                out=num[:, t, :], in0=y_ps[t][:], scalar=gn_t[:, t : t + 1], in1=pa[:, t, :], op0=ALU.mult, op1=ALU.mult
+            )
+            nc.vector.tensor_tensor(out=den[:, t, :], in0=y_sq[:, t, :], in1=pa_sq[:, t, :], op=ALU.add)
+
+        w4_bf = sb("w4_bf", [P, 512 * PACK], BF16)
+        cast(w4_bf, w4_raw, False, 0, 64)
+        w4_q = quantize(w4_bf[:], "w4")
+        w3_bf = sb("w3_bf", [P, 512 * PACK], BF16)
+        cast(w3_bf, w3_raw, False, 0, 128)
+        w3_q = quantize(w3_bf[:], "w3")
+
+        h_early = [psum.tile([P, 256], F32, name="he%d" % t, tag="bank%d" % t) for t in range(PACK)]
+        h_late = [psum.tile([P, 256], F32, name="hl%d" % t, tag="bank%d" % (PACK + t)) for t in range(PACK)]
+        for t in range(PACK):
+            product(h_early[t][:], w4_q, block(t), z2_q, slice(0, 256), True, False)
+            product(h_late[t][:], w4_q, block(t), z2_q, slice(256, S), True, False)
+        for c in range(4):
+            root = sb("root%d" % c, [P, PACK, P], F32)
+            recip = sb("recip%d" % c, [P, PACK, P], F32)
+            z_bf = sb("z_bf%d" % c, [P, P * PACK], BF16)
+            nc.scalar.activation(out=root[:], in_=den[:, :, block(c)], func=ACT.Abs_reciprocal_sqrt, scale=0.5, bias=0.25)
+            square("VSSS"[c] == "V", recip[:], root[:], root[:])
+            weave(z_bf[:], num[:, :, block(c)], recip[:])
+            z_q = quantize(z_bf[:], "z%d" % c)
+            for t in range(PACK):
+                acc = (h_early if c < 2 else h_late)[t][:, block(c % 2)]
+                product(acc, w3_q, block(t), z_q, block(0), False, c % 2 == 1)
+        twin = sb("twin", [P, S], F32)
+        for t in range(PACK):
+            evacuate("SSSS"[t] == "V", win_a[t][:, :256], h_early[t][:])
+            if t == 0:
+                nc.scalar.activation(out=twin[:, :256], in_=h_early[t][:], func=ACT.Copy, scale=0.75)
 
         for t in range(PACK):
-            g3 = sb("g3_%d" % t, [P, S], F32)
             g4 = sb("g4_%d" % t, [P, S], F32)
             first = sb("first_%d" % t, [P, S], F32)
             second = sb("second_%d" % t, [P, S], F32)
             res = sb("res_%d" % t, [P, S], F32)
-            nc.scalar.copy(out=win_a[t][:, :S], in_=h_ps[t][:])
+            evacuate("SSVV"[t] == "V", win_a[t][:, 256:S], h_late[t][:])
             if t == 0:
-                nc.vector.tensor_copy(out=g4[:], in_=win_a[t][:].indirect(n4_t[:]))
+                nc.scalar.activation(out=twin[:, 256:], in_=h_late[t][:], func=ACT.Copy, scale=0.75)
+            gather(False, g4[:], win_a[t], n4_t[:])
+            if t == 0:
+                nc.vector.tensor_tensor(out=first[:], in0=win_a[t][:].indirect(n3_t[:]), in1=twin[:], op=ALU.mult)
             else:
-                nc.scalar.activation(out=g4[:], in_=win_a[t][:].indirect(n4_t[:]), func=ACT.Copy)
-            nc.scalar.activation(out=g3[:], in_=win_a[t][:].indirect(n3_t[:]), func=ACT.Copy)
+                g3 = sb("g3_%d" % t, [P, S], F32)
+                gather(False, g3[:], win_a[t], n3_t[:])
             nc.vector.tensor_tensor(out=second[:], in0=win_a[t][:].indirect(n5_t[:]), in1=g4[:], op=ALU.mult)
-            nc.vector.scalar_tensor_tensor(out=first[:], in0=h_ps[t][:], scalar=0.75, in1=g3[:], op0=ALU.mult, op1=ALU.mult)
-            nc.vector.scalar_tensor_tensor(out=res[:], in0=second[:], scalar=0.75, in1=first[:], op0=ALU.mult, op1=ALU.add)
-            nc.sync.dma_start(out=out[P * t : P * (t + 1), :], in_=res[:])
+            pieces = [(0, 256), (256, 512)] if t == PACK - 1 else [(0, S)]
+            for a, b in pieces:
+                if t > 0:
+                    nc.vector.scalar_tensor_tensor(
+                        out=first[:, a:b], in0=win_a[t][:, a:b], scalar=0.75, in1=g3[:, a:b], op0=ALU.mult, op1=ALU.mult
+                    )
+                nc.vector.scalar_tensor_tensor(
+                    out=res[:, a:b], in0=second[:, a:b], scalar=0.75, in1=first[:, a:b], op0=ALU.mult, op1=ALU.add
+                )
+                nc.sync.dma_start(out=out[block(t), a:b], in_=res[:, a:b])

@@ -47,12 +47,11 @@ def tile_picked_hjoinharmnormdot_none_p_kernel(
         offs_t = load_list("offs_t", offs)
         n2_t = load_list("n2_t", n2)
         n1_t = load_list("n1_t", n1)
+        n3_t = load_list("n3_t", n3)
         xw = sb("xw", [P, T], I32)
         nc.sync.dma_start(out=xw[:], in_=x_words[0].rearrange("p n t -> p (n t)").bitcast(I32))
         w2_lo = load_weight("w2_lo", w2[:, :256], "raw_c")
         w2_hi = load_weight("w2_hi", w2[:, 256:], "raw_a")
-        w1_raw = load_weight("w1_raw", w1, "raw_b")
-        n3_t = load_list("n3_t", n3)
         n4_t = load_list("n4_t", n4)
         n5_t = load_list("n5_t", n5)
         gn_t = sb("gn_t", [P, PACK], F32)
@@ -70,17 +69,20 @@ def tile_picked_hjoinharmnormdot_none_p_kernel(
         nc.vector.memset(warm_in[:], 1.0)
         nc.scalar.activation(out=warm_out[:], in_=warm_in[:], func=ACT.Abs_reciprocal_sqrt)
 
-        def cast(grouped, raw, dealt, first, cut):
-            if dealt:
-                dst = grouped[:].rearrange("p (t m j) -> p m j t", t=PACK, j=PACK)
-            else:
-                dst = grouped[:].rearrange("p (m t j) -> p m j t", t=PACK, j=PACK)
+        def cast(grouped, raw, cut):
+            dst = grouped[:].rearrange("p (m i j) -> p m j i", i=2, j=PACK)
+            src = raw[:].rearrange("p j (m i) -> p m j i", i=2)
+            if cut > 0:
+                nc.vector.tensor_copy(out=dst[:, :cut], in_=src[:, :cut])
+            for a in range(cut, 256, 64):
+                nc.scalar.copy(out=dst[:, a : a + 64], in_=src[:, a : a + 64])
+
+        def cast_dealt(on_vector, grouped, raw, first):
+            dst = grouped[:].rearrange("p (t m j) -> p m j t", t=PACK, j=PACK)
             src = raw[:].rearrange("p j (m t) -> p m j t", t=PACK)
             groups = src.shape[1]
-            if cut > 0:
-                nc.vector.tensor_copy(out=dst[:, first : first + cut], in_=src[:, :cut])
-            for a in range(cut, groups, 32):
-                nc.scalar.copy(out=dst[:, first + a : first + a + 32], in_=src[:, a : a + 32])
+            for t in (0, 2):
+                evacuate(on_vector, dst[:, first : first + groups, :, t : t + 2], src[:, :, :, t : t + 2])
 
         def quantize(grouped, name):
             width = grouped.shape[1] // PACK
@@ -113,9 +115,9 @@ def tile_picked_hjoinharmnormdot_none_p_kernel(
 
         def weave(dst, left, right):
             nc.vector.tensor_tensor(
-                out=dst.rearrange("p (c i t) -> p c t i", i=4, t=PACK),
-                in0=left.rearrange("p t (c i) -> p c t i", i=4),
-                in1=right.rearrange("p t (c i) -> p c t i", i=4),
+                out=dst.rearrange("p (c i t) -> p c t i", i=2, t=PACK),
+                in0=left.rearrange("p t (c i) -> p c t i", i=2),
+                in1=right.rearrange("p t (c i) -> p c t i", i=2),
                 op=ALU.mult,
             )
 
@@ -139,42 +141,51 @@ def tile_picked_hjoinharmnormdot_none_p_kernel(
                     out=dst[:, a : a + 128], in0=src[:, a : a + 128], scalar1=1.0, scalar2=0.0, op0=ALU.mult, op1=ALU.add
                 )
 
-        picked_bytes = sb("picked_bytes", [P, 2 * S], U8)
-        nc.vector.tensor_copy(out=picked_bytes[:, :S], in_=xs[:].indirect(hz_t[:]))
-        nc.vector.tensor_copy(out=picked_bytes[:, S:], in_=xs[:].indirect(offs_t[:]))
-        x_planes = sb("x_planes", [P, 2 * S], U8)
-        nc.vector.tensor_copy(out=x_planes[:].bitcast(I32), in_=picked_bytes[:].bitcast(I32))
-        for r in (1, 2, 3):
-            nc.scalar.dma_start(out=x_planes[r:P:32, :].bitcast(I32), in_=picked_bytes[8 * r : P : 32, :].bitcast(I32))
+        def pick_bytes(name, offsets):
+            picked = sb(name, [P, S], U8)
+            nc.vector.tensor_copy(out=picked[:], in_=xs[:].indirect(offsets[:]))
+            return picked
+
+        def place_rows(name, picked, queue):
+            plane = sb(name, [P, S], U8)
+            nc.vector.tensor_copy(out=plane[:].bitcast(I32), in_=picked[:].bitcast(I32))
+            for r in (1, 2, 3):
+                queue.dma_start(out=plane[r:P:32, :].bitcast(I32), in_=picked[8 * r : P : 32, :].bitcast(I32))
+            return plane
+
+        hz_plane = place_rows("hz_plane", pick_bytes("hz_bytes", hz_t), nc.scalar)
+        tok_bytes = pick_bytes("tok_bytes", offs_t)
+        w1_raw = load_weight("w1_raw", w1, "xs")
+        tok_plane = place_rows("tok_plane", tok_bytes, nc.sync)
         hz_words = sb("hz_words", [P, S], U32)
         nc.vector.tensor_copy(out=hz_words[:], in_=xw[:].bitcast(U32).indirect(hz_t[:]))
         w2_bf = sb("w2_bf", [P, 512 * PACK], BF16)
-        cast(w2_bf, w2_lo, True, 0, 0)
-        cast(w2_bf, w2_hi, True, 64, 0)
+        cast_dealt(False, w2_bf, w2_lo, 0)
+        cast_dealt(False, w2_bf, w2_hi, 64)
+        w4_raw = load_weight("w4_raw", w4, "raw_c")
         w3_raw = load_weight("w3_raw", w3, "raw_a")
         d_ps = [psum.tile([P, S], F32, name="d%d" % t, tag="bank%d" % (PACK + t)) for t in range(PACK)]
         for t in range(PACK):
             w2_q = quantize(w2_bf[:, 512 * t : 512 * (t + 1)], "w2_%d" % t)
-            product(d_ps[t][:], w2_q, block(0), (hz_words, x_planes[:, :S]), every, True, True)
+            product(d_ps[t][:], w2_q, block(0), (hz_words, hz_plane), every, True, True)
 
         tok_words = sb("tok_words", [P, S], U32)
         nc.vector.tensor_copy(out=tok_words[:], in_=xw[:].bitcast(U32).indirect(offs_t[:]))
         w1_bf = sb("w1_bf", [P, 512 * PACK], BF16)
-        cast(w1_bf, w1_raw, True, 0, P)
+        cast_dealt(True, w1_bf, w1_raw, 0)
         w1_q = quantize(w1_bf[:], "w1")
-        w4_raw = load_weight("w4_raw", w4, "raw_b")
 
         y_ps = [psum.tile([P, S], F32, name="y%d" % t, tag="bank%d" % t) for t in range(PACK)]
         for t in range(PACK):
-            product(y_ps[t][:], w1_q, block(t), (tok_words, x_planes[:, S:]), every, True, True)
+            product(y_ps[t][:], w1_q, block(t), (tok_words, tok_plane), every, True, True)
 
         d_abs = sb("d_abs", [P, PACK, S], F32)
-        s_g = sb("s_g", [P, PACK, S], F32)
+        s_g = sb("s_g", [P, PACK, S], F32, tag="w1_bf")
         d_s = sb("d_s", [P, PACK, S], F32)
         for t in range(PACK):
             nc.scalar.activation(out=d_abs[:, t, :], in_=d_ps[t][:], func=ACT.Abs)
             nc.scalar.activation(out=win_b[t][:, :S], in_=d_abs[:, t, :], func=ACT.Abs_reciprocal_sqrt, bias=0.5)
-            gather("SVVV"[t] == "V", s_g[:, t, :], win_b[t], n2_t[:])
+            gather("VVVS"[t] == "V", s_g[:, t, :], win_b[t], n2_t[:])
             nc.vector.scalar_tensor_tensor(
                 out=d_s[:, t, :], in0=d_ps[t][:], scalar=gm_t[:, t : t + 1], in1=s_g[:, t, :], op0=ALU.mult, op1=ALU.mult
             )
@@ -191,7 +202,7 @@ def tile_picked_hjoinharmnormdot_none_p_kernel(
         for t in range(PACK):
             evacuate("SSSS"[t] == "V", win_a[t][:, :S], y_ps[t][:])
             gather("SSSS"[t] == "V", pa[:, t, :], win_a[t], n1_t[:])
-            square("SSSS"[t] == "V", y_sq[:, t, :], y_ps[t][:], win_a[t][:, :S])
+            square("VVSS"[t] == "V", y_sq[:, t, :], y_ps[t][:], win_a[t][:, :S])
             square("SSSS"[t] == "V", pa_sq[:, t, :], pa[:, t, :], pa[:, t, :])
             nc.vector.scalar_tensor_tensor(
                 out=num[:, t, :], in0=y_ps[t][:], scalar=gn_t[:, t : t + 1], in1=pa[:, t, :], op0=ALU.mult, op1=ALU.mult
@@ -199,10 +210,10 @@ def tile_picked_hjoinharmnormdot_none_p_kernel(
             nc.vector.tensor_tensor(out=den[:, t, :], in0=y_sq[:, t, :], in1=pa_sq[:, t, :], op=ALU.add)
 
         w4_bf = sb("w4_bf", [P, 512 * PACK], BF16)
-        cast(w4_bf, w4_raw, False, 0, 64)
+        cast_pool(w4_bf, w4_raw)
         w4_q = quantize(w4_bf[:], "w4")
         w3_bf = sb("w3_bf", [P, 512 * PACK], BF16)
-        cast(w3_bf, w3_raw, False, 0, 128)
+        cast_pool(w3_bf, w3_raw)
         w3_q = quantize(w3_bf[:], "w3")
 
         h_early = [psum.tile([P, 256], F32, name="he%d" % t, tag="bank%d" % t) for t in range(PACK)]
@@ -232,7 +243,7 @@ def tile_picked_hjoinharmnormdot_none_p_kernel(
             first = sb("first_%d" % t, [P, S], F32)
             second = sb("second_%d" % t, [P, S], F32)
             res = sb("res_%d" % t, [P, S], F32)
-            evacuate("SSVV"[t] == "V", win_a[t][:, 256:S], h_late[t][:])
+            evacuate("SVVV"[t] == "V", win_a[t][:, 256:S], h_late[t][:])
             if t == 0:
                 nc.scalar.activation(out=twin[:, 256:], in_=h_late[t][:], func=ACT.Copy, scale=0.75)
             gather(False, g4[:], win_a[t], n4_t[:])

from contextlib import ExitStack

import concourse.mybir as mybir

K, T, S, H, N = 512, 2048, 512, 512, 512
FLOPS = 4 * 2 * 512 * 512 * 512

F32 = mybir.dt.float32
BF16 = mybir.dt.bfloat16
I32 = mybir.dt.int32
U32 = mybir.dt.uint32
U16 = mybir.dt.uint16
U8 = mybir.dt.uint8
FP8X4 = mybir.dt.float8_e4m3fn_x4
ACT = mybir.ActivationFunctionType
ALU = mybir.AluOpType

P = 128
PACK = 4
WINDOW = 704


def tile_picked_hjoinharmnormdot_none_p_kernel(
    tc, x_words, x_scales, w1, w2, gn, gm, w3, w4, offs, hz, n1, n2, n3, n4, n5, out
):
    nc = tc.nc
    with ExitStack() as ctx:
        keep = ctx.enter_context(tc.tile_pool(name="keep", bufs=1))
        psum = ctx.enter_context(tc.psum_pool(name="psum", bufs=1))

        def sb(name, shape, dtype, tag=None):
            return keep.tile(shape, dtype, name=name, tag=tag or name, align_bytes=64)

        def load_list(name, src):
            tile = keep.tile([P, S // 16], U16, name=name, tag=name)
            nc.sync.dma_start(tile[:], src)
            return tile

        def load_weight(name, src, tag):
            raw = sb(name, [P, PACK, src.shape[1]], F32, tag=tag)
            nc.sync.dma_start(out=raw[:], in_=src.rearrange("(p j) c -> p j c", j=PACK))
            return raw

        xs = sb("xs", [P, T], U8)
        nc.sync.dma_start(out=xs[:].bitcast(I32), in_=x_scales[0].bitcast(I32).unsqueeze(1).to_broadcast([16, 8, T // 4]))
        hz_t = load_list("hz_t", hz)
        offs_t = load_list("offs_t", offs)
        n2_t = load_list("n2_t", n2)
        n1_t = load_list("n1_t", n1)
        n3_t = load_list("n3_t", n3)
        xw = sb("xw", [P, T], I32)
        nc.sync.dma_start(out=xw[:], in_=x_words[0].rearrange("p n t -> p (n t)").bitcast(I32))
        w2_lo = load_weight("w2_lo", w2[:, :256], "raw_c")
        w2_hi = load_weight("w2_hi", w2[:, 256:], "raw_a")
        n4_t = load_list("n4_t", n4)
        n5_t = load_list("n5_t", n5)
        gn_t = sb("gn_t", [P, PACK], F32)
        gm_t = sb("gm_t", [P, PACK], F32)
        nc.gpsimd.dma_start(out=gm_t[:], in_=gm.rearrange("(p t) o -> p (t o)", t=PACK))
        nc.gpsimd.dma_start(out=gn_t[:], in_=gn.rearrange("(p t) o -> p (t o)", t=PACK))

        win_a = [sb("win_a%d" % t, [P, WINDOW], F32) for t in range(PACK)]
        win_b = [sb("win_b%d" % t, [P, WINDOW], F32) for t in range(PACK)]
        for w in win_a + win_b:
            nc.vector.memset(w[:, S:], 0.0)

        warm_in = sb("warm_in", [P, 8], F32)
        warm_out = sb("warm_out", [P, 8], F32)
        nc.vector.memset(warm_in[:], 1.0)
        nc.scalar.activation(out=warm_out[:], in_=warm_in[:], func=ACT.Abs_reciprocal_sqrt)

        def cast(grouped, raw, cut):
            dst = grouped[:].rearrange("p (m i j) -> p m j i", i=2, j=PACK)
            src = raw[:].rearrange("p j (m i) -> p m j i", i=2)
            if cut > 0:
                nc.vector.tensor_copy(out=dst[:, :cut], in_=src[:, :cut])
            for a in range(cut, 256, 64):
                nc.scalar.copy(out=dst[:, a : a + 64], in_=src[:, a : a + 64])

        def cast_dealt(on_vector, grouped, raw, first):
            dst = grouped[:].rearrange("p (t m j) -> p m j t", t=PACK, j=PACK)
            src = raw[:].rearrange("p j (m t) -> p m j t", t=PACK)
            groups = src.shape[1]
            for t in (0, 2):
                evacuate(on_vector, dst[:, first : first + groups, :, t : t + 2], src[:, :, :, t : t + 2])

        def quantize(grouped, name):
            width = grouped.shape[1] // PACK
            codes = sb(name + "_codes", [P, width], U32)
            scales = sb(name + "_scales", [P, width], U8)
            nc.vector.quantize_mx(out=codes[:].bitcast(FP8X4), scales=scales[:], in_=grouped)
            return codes, scales

        def product(acc, weight, wcols, moving, mcols, start, stop):
            nc.tensor.matmul_mx(
                out=acc,
                lhsT=weight[0][:, wcols].bitcast(FP8X4),
                lhsT_scale=weight[1][:, wcols],
                rhs=moving[0][:, mcols].bitcast(FP8X4),
                rhs_scale=moving[1][:, mcols],
                start=start,
                stop=stop,
            )

        def block(t):
            return slice(P * t, P * (t + 1))

        every = slice(0, S)

        def gather(on_vector, dst, window, offsets):
            if on_vector:
                nc.vector.tensor_copy(out=dst, in_=window[:].indirect(offsets))
            else:
                nc.scalar.activation(out=dst, in_=window[:].indirect(offsets), func=ACT.Copy)

        def weave(dst, left, right):
            nc.vector.tensor_tensor(
                out=dst.rearrange("p (c i t) -> p c t i", i=2, t=PACK),
                in0=left.rearrange("p t (c i) -> p c t i", i=2),
                in1=right.rearrange("p t (c i) -> p c t i", i=2),
                op=ALU.mult,
            )

        def square(on_vector, dst, src, twin):
            if on_vector:
                nc.vector.tensor_tensor(out=dst, in0=src, in1=twin, op=ALU.mult)
            else:
                nc.scalar.activation(out=dst, in_=src, func=ACT.Square)

        def evacuate(on_vector, dst, src):
            if on_vector:
                nc.vector.tensor_copy(out=dst, in_=src)
            else:
                nc.scalar.copy(out=dst, in_=src)

        def cast_pool(grouped, raw):
            dst = grouped[:].rearrange("p (c j) -> p c j", j=PACK)
            src = raw[:].rearrange("p j c -> p c j")
            for a in range(0, 512, 128):
                nc.gpsimd.tensor_scalar(
                    out=dst[:, a : a + 128], in0=src[:, a : a + 128], scalar1=1.0, scalar2=0.0, op0=ALU.mult, op1=ALU.add
                )

        def pick_bytes(name, offsets):
            picked = sb(name, [P, S], U8)
            nc.vector.tensor_copy(out=picked[:], in_=xs[:].indirect(offsets[:]))
            return picked

        def place_rows(name, picked, queue):
            plane = sb(name, [P, S], U8)
            nc.vector.tensor_copy(out=plane[:].bitcast(I32), in_=picked[:].bitcast(I32))
            for r in (1, 2, 3):
                queue.dma_start(out=plane[r:P:32, :].bitcast(I32), in_=picked[8 * r : P : 32, :].bitcast(I32))
            return plane

        hz_plane = place_rows("hz_plane", pick_bytes("hz_bytes", hz_t), nc.scalar)
        tok_bytes = pick_bytes("tok_bytes", offs_t)
        w1_raw = load_weight("w1_raw", w1, "xs")
        tok_plane = place_rows("tok_plane", tok_bytes, nc.sync)
        hz_words = sb("hz_words", [P, S], U32)
        nc.vector.tensor_copy(out=hz_words[:], in_=xw[:].bitcast(U32).indirect(hz_t[:]))
        w2_bf = sb("w2_bf", [P, 512 * PACK], BF16)
        cast_dealt(False, w2_bf, w2_lo, 0)
        cast_dealt(False, w2_bf, w2_hi, 64)
        w4_raw = load_weight("w4_raw", w4, "raw_c")
        w3_raw = load_weight("w3_raw", w3, "raw_a")
        d_ps = [psum.tile([P, S], F32, name="d%d" % t, tag="bank%d" % (PACK + t)) for t in range(PACK)]
        for t in range(PACK):
            w2_q = quantize(w2_bf[:, 512 * t : 512 * (t + 1)], "w2_%d" % t)
            product(d_ps[t][:], w2_q, block(0), (hz_words, hz_plane), every, True, True)

        tok_words = sb("tok_words", [P, S], U32)
        nc.vector.tensor_copy(out=tok_words[:], in_=xw[:].bitcast(U32).indirect(offs_t[:]))
        w1_bf = sb("w1_bf", [P, 512 * PACK], BF16)
        cast_dealt(True, w1_bf, w1_raw, 0)
        w1_q = quantize(w1_bf[:], "w1")

        y_ps = [psum.tile([P, S], F32, name="y%d" % t, tag="bank%d" % t) for t in range(PACK)]
        for t in range(PACK):
            product(y_ps[t][:], w1_q, block(t), (tok_words, tok_plane), every, True, True)

        d_abs = sb("d_abs", [P, PACK, S], F32)
        s_g = sb("s_g", [P, PACK, S], F32, tag="w1_bf")
        d_s = sb("d_s", [P, PACK, S], F32)
        for t in range(PACK):
            nc.scalar.activation(out=d_abs[:, t, :], in_=d_ps[t][:], func=ACT.Abs)
            nc.scalar.activation(out=win_b[t][:, :S], in_=d_abs[:, t, :], func=ACT.Abs_reciprocal_sqrt, bias=0.5)
            gather("VVVS"[t] == "V", s_g[:, t, :], win_b[t], n2_t[:])
            nc.vector.scalar_tensor_tensor(
                out=d_s[:, t, :], in0=d_ps[t][:], scalar=gm_t[:, t : t + 1], in1=s_g[:, t, :], op0=ALU.mult, op1=ALU.mult
            )
        z2_bf = sb("z2_bf", [P, S * PACK], BF16)
        for c in range(4):
            weave(z2_bf[:, 512 * c : 512 * (c + 1)], d_s[:, :, block(c)], s_g[:, :, block(c)])
        z2_q = quantize(z2_bf[:], "z2")

        pa = sb("pa", [P, PACK, S], F32)
        y_sq = sb("y_sq", [P, PACK, S], F32)
        pa_sq = sb("pa_sq", [P, PACK, S], F32)
        num = sb("num", [P, PACK, S], F32)
        den = sb("den", [P, PACK, S], F32)
        for t in range(PACK):
            evacuate("SSSS"[t] == "V", win_a[t][:, :S], y_ps[t][:])
            gather("SSSS"[t] == "V", pa[:, t, :], win_a[t], n1_t[:])
            square("VVSS"[t] == "V", y_sq[:, t, :], y_ps[t][:], win_a[t][:, :S])
            square("SSSS"[t] == "V", pa_sq[:, t, :], pa[:, t, :], pa[:, t, :])
            nc.vector.scalar_tensor_tensor(
                out=num[:, t, :], in0=y_ps[t][:], scalar=gn_t[:, t : t + 1], in1=pa[:, t, :], op0=ALU.mult, op1=ALU.mult
            )
            nc.vector.tensor_tensor(out=den[:, t, :], in0=y_sq[:, t, :], in1=pa_sq[:, t, :], op=ALU.add)

        w4_bf = sb("w4_bf", [P, 512 * PACK], BF16)
        cast_pool(w4_bf, w4_raw)
        w4_q = quantize(w4_bf[:], "w4")
        w3_bf = sb("w3_bf", [P, 512 * PACK], BF16)
        cast_pool(w3_bf, w3_raw)
        w3_q = quantize(w3_bf[:], "w3")

        h_early = [psum.tile([P, 256], F32, name="he%d" % t, tag="bank%d" % t) for t in range(PACK)]
        h_late = [psum.tile([P, 256], F32, name="hl%d" % t, tag="bank%d" % (PACK + t)) for t in range(PACK)]
        for t in range(PACK):
            product(h_early[t][:], w4_q, block(t), z2_q, slice(0, 256), True, False)
            product(h_late[t][:], w4_q, block(t), z2_q, slice(256, S), True, False)
        for c in range(4):
            root = sb("root%d" % c, [P, PACK, P], F32)
            recip = sb("recip%d" % c, [P, PACK, P], F32)
            z_bf = sb("z_bf%d" % c, [P, P * PACK], BF16)
            nc.scalar.activation(out=root[:], in_=den[:, :, block(c)], func=ACT.Abs_reciprocal_sqrt, scale=0.5, bias=0.25)
            square("VSSS"[c] == "V", recip[:], root[:], root[:])
            weave(z_bf[:], num[:, :, block(c)], recip[:])
            z_q = quantize(z_bf[:], "z%d" % c)
            for t in range(PACK):
                acc = (h_early if c < 2 else h_late)[t][:, block(c % 2)]
                product(acc, w3_q, block(t), z_q, block(0), False, c % 2 == 1)
        twin = sb("twin", [P, S], F32)
        for t in range(PACK):
            evacuate("SSSS"[t] == "V", win_a[t][:, :256], h_early[t][:])
            if t == 0:
                nc.scalar.activation(out=twin[:, :256], in_=h_early[t][:], func=ACT.Copy, scale=0.75)

        for t in range(PACK):
            g4 = sb("g4_%d" % t, [P, S], F32)
            first = sb("first_%d" % t, [P, S], F32)
            second = sb("second_%d" % t, [P, S], F32)
            res = sb("res_%d" % t, [P, S], F32)
            evacuate("SVVV"[t] == "V", win_a[t][:, 256:S], h_late[t][:])
            if t == 0:
                nc.scalar.activation(out=twin[:, 256:], in_=h_late[t][:], func=ACT.Copy, scale=0.75)
            gather(False, g4[:], win_a[t], n4_t[:])
            if t == 0:
                nc.vector.tensor_tensor(out=first[:], in0=win_a[t][:].indirect(n3_t[:]), in1=twin[:], op=ALU.mult)
            else:
                g3 = sb("g3_%d" % t, [P, S], F32)
                gather(False, g3[:], win_a[t], n3_t[:])
            nc.vector.tensor_tensor(out=second[:], in0=win_a[t][:].indirect(n5_t[:]), in1=g4[:], op=ALU.mult)
            pieces = [(0, 256), (256, 512)] if t == PACK - 1 else [(0, S)]
            for a, b in pieces:
                if t > 0:
                    nc.vector.scalar_tensor_tensor(
                        out=first[:, a:b], in0=win_a[t][:, a:b], scalar=0.75, in1=g3[:, a:b], op0=ALU.mult, op1=ALU.mult
                    )
                nc.vector.scalar_tensor_tensor(
                    out=res[:, a:b], in0=second[:, a:b], scalar=0.75, in1=first[:, a:b], op0=ALU.mult, op1=ALU.add
                )
                nc.sync.dma_start(out=out[block(t), a:b], in_=res[:, a:b])
